import numpy as np
import ml_dtypes


def mxq(x, axis, fmt="e4m3"):
    dtype, down = {"e4m3": (ml_dtypes.float8_e4m3fn, 7), "e5m2": (ml_dtypes.float8_e5m2, 14)}[fmt]
    v = np.moveaxis(np.asarray(x, np.float32).astype(ml_dtypes.bfloat16).astype(np.float64), axis, -1)
    blocks = v.reshape(v.shape[:-1] + (-1, 32))
    amax = np.abs(blocks).max(-1, keepdims=True)
    byte = np.maximum(np.where(amax > 0, np.frexp(amax)[1] - 1 + 127, 0) - down, 1)
    scale = np.exp2(byte - 127.0)
    codes = (blocks / scale).astype(np.float32).astype(dtype).astype(np.float64)
    return np.moveaxis((codes * scale).reshape(v.shape), -1, axis)


WIDE = False


def mx_kscale(k):
    if not WIDE:
        return np.ones(k)
    levels = np.array([10, -10, 5, -5, 0])
    if k % 512:
        return np.exp2(np.random.permutation(np.resize(levels, k // 32))).repeat(32)
    a = np.empty((k // 512, 16))
    for p in range(k // 512):
        a[p, :8] = np.random.permutation(np.resize(levels, 8))
        for g in range(8):
            far = levels[np.abs(levels - a[p, g]) >= 10]
            a[p, g + 8] = far[np.random.randint(len(far))]
    return np.exp2(a.ravel()).repeat(32)


def f64(x):
    return np.asarray(x).astype(np.float64)


def striped(idx):
    return np.tile(np.asarray(idx).reshape(-1, 16).T, (8, 1)).astype(np.uint16)


def unstriped(offs):
    return offs[:16].T.reshape(-1).astype(np.int64)


E2M1 = np.array([0.0, 0.5, 1.0, 1.5, 2.0, 3.0, 4.0, 6.0, -0.0, -0.5, -1.0, -1.5, -2.0, -3.0, -4.0, -6.0])


def pack_weight(w, fmt):
    k, n = w.shape
    w = f64(np.asarray(w, np.float32).astype(ml_dtypes.bfloat16)).reshape(k // 32, 32, n)
    amax = np.abs(w).max(1)
    if fmt == "e4m3":
        byte = np.frexp(amax)[1] - 1 + 127 - 7
    else:
        mant, ex = np.frexp(amax / 6.0)
        byte = np.where(mant > 0.5, ex, ex - 1) + 127
    byte = np.clip(np.where(amax > 0, byte, 1), 1, 254)
    scaled = (w * np.exp2(127.0 - byte)[:, None, :]).reshape(k, n).astype(np.float32)
    by_word = np.ascontiguousarray(scaled.reshape(k // 512, 128, 4, n).transpose(0, 1, 3, 2))
    if fmt == "e4m3":
        words = by_word.astype(ml_dtypes.float8_e4m3fn).view(np.uint8)
    else:
        c = by_word.astype(ml_dtypes.float4_e2m1fn).view(np.uint8) & 0xF
        words = (c[..., 0::2] | (c[..., 1::2] << 4)).reshape(k // 512, 128, 2 * n)
    return np.ascontiguousarray(words), np.ascontiguousarray(byte.astype(np.uint8).reshape(k // 512, 16, n))


def unpack_weight(words, scales, fmt):
    g, _, n = scales.shape
    words = np.ascontiguousarray(words).reshape(g, 128, n, -1)
    if fmt == "e4m3":
        vals = words.view(ml_dtypes.float8_e4m3fn).astype(np.float64)
    else:
        nib = np.empty((g, 128, n, 4), np.uint8)
        nib[..., 0::2] = words & 0xF
        nib[..., 1::2] = words >> 4
        vals = E2M1[nib]
    vals = vals * np.repeat(np.exp2(scales.astype(np.float64) - 127.0), 8, axis=1)[..., None]
    return vals.transpose(0, 1, 3, 2).reshape(g * 512, n)


def sigmoid(v):
    return 1.0 / (1.0 + np.exp(-v))


D, E, T, I, Q = 512, 512, 2048, 512, 128


def setup_inputs():
    n = np.random.standard_normal
    idx = np.random.permutation(T)[:I]
    fd = mx_kscale(D)
    fe = mx_kscale(E)
    keysp = pack_weight(n((D, T)) / fd[:, None], "e2m1")
    valsp = pack_weight(n((E, T)) / fe[:, None], "e2m1")
    return {
        "query": (n((D, Q)) * 0.5 / np.sqrt(D) * fd[:, None]).astype(np.float32),
        "query2": (n((D, Q)) * 0.6 / np.sqrt(D) * fd[:, None]).astype(np.float32),
        "keys_words": keysp[0],
        "keys_scales": keysp[1],
        "age": np.tile(np.random.uniform(0.0, 2.0, T), (128, 1)).astype(np.float32),
        "grace": (np.random.uniform(0.7, 1.5, (Q, 1))).astype(np.float32),
        "gout": (n((E, Q)) * 1 / np.sqrt(E) * fe[:, None]).astype(np.float32),
        "vals_words": valsp[0],
        "vals_scales": valsp[1],
        "size": (np.random.uniform(0.5, 2.0, (1, I))).astype(np.float32),
        "dquery2": (n((D, Q)) * 1.0 / np.sqrt(D) * fd[:, None]).astype(np.float32),
        "base": (0.5 * n((Q, T))).astype(np.float32),
        "offs": striped(idx),
    }


def reference(query, query2, keys_words, keys_scales, age, grace, gout, vals_words, vals_scales, size, dquery2, base, offs):
    idx = unstriped(offs)
    keysu = unpack_weight(keys_words, keys_scales, "e2m1")
    valsu = unpack_weight(vals_words, vals_scales, "e2m1")
    queryq = mxq(f64(query), 0, "e4m3")
    keysidxg = keysu[:, idx]
    a = queryq.T @ keysidxg
    query2q = mxq(f64(query2), 0, "e4m3")
    b = query2q.T @ keysidxg
    dquery2q = mxq(f64(dquery2), 0, "e4m3")
    tb = dquery2q.T @ keysidxg
    r = np.exp(a - np.max(a, axis=1, keepdims=True))
    gt = sigmoid((b + f64(grace) - f64(age)[:1][:, idx]) * 3.0)
    p = r * gt
    z = np.sum(p, axis=1, keepdims=True)
    goutq = mxq(f64(gout), 0, "e4m3")
    valsidxg = valsu[:, idx]
    c0 = goutq.T @ valsidxg
    dz = np.sum(c0 * p * f64(size) / np.square(z) * (-1.0), axis=1, keepdims=True)
    dp = c0 / z * f64(size) + dz
    dgt = dp * r
    tgt = tb * 3.0 * gt * (1.0 - gt)
    tp = tgt * r
    tz = np.sum(tp, axis=1, keepdims=True)
    tdz = np.sum((tp * f64(size) * c0 - tz * z * 2.0 * c0 * p * f64(size) / np.square(z)) / np.square(z) * (-1.0), axis=1, keepdims=True)
    tdp = tz * c0 / np.square(z) * (-1.0) * f64(size) + tdz
    tdgt = tdp * r
    tdb = ((tdgt * gt + tgt * dgt) * (1.0 - gt) + tgt * (-1.0) * dgt * gt) * 3.0
    gs = tdb * 512.0
    gf = np.zeros((Q, T))
    gf[:, idx] = gs
    y = f64(base) + gf
    return y

@@ -1,0 +1,196 @@
+from contextlib import ExitStack
+
+import concourse.mybir as mybir
+from concourse.masks import make_identity
+
+D, T, I, Q = 512, 2048, 512, 128
+P = 128
+PACK = 4
+STORE_EDGES = (0, 256, 768, 1280, 1792, 2048)
+
+FLOPS = 4 * 2 * D * Q * I
+
+F32 = mybir.dt.float32
+BF16 = mybir.dt.bfloat16
+I32 = mybir.dt.int32
+U32 = mybir.dt.uint32
+U16 = mybir.dt.uint16
+U8 = mybir.dt.uint8
+FP8X4 = mybir.dt.float8_e4m3fn_x4
+FP4X4 = mybir.dt.float4_e2m1fn_x4
+ALU = mybir.AluOpType
+ACT = mybir.ActivationFunctionType
+
+
+def tile_attend_hvsoftlives_b_s_kernel(
+    tc, query, query2, keys_words, keys_scales, age, grace, gout, vals_words, vals_scales, size, dquery2, base, offs, out
+):
+    nc = tc.nc
+    with ExitStack() as ctx:
+        sb = ctx.enter_context(tc.tile_pool(name="sb", bufs=1))
+        ps = ctx.enter_context(tc.psum_pool(name="ps", bufs=1))
+
+        def wide(name):
+            return sb.tile([P, I], F32, name=name)
+
+        def column(name):
+            return sb.tile([P, 1], F32, name=name)
+
+        offsets = sb.tile([P, I // 16], U16, name="offsets")
+        nc.sync.dma_start(offsets[:], offs)
+
+        key_bytes = sb.tile([P, T], U8, name="key_bytes")
+        val_bytes = sb.tile([P, T], U8, name="val_bytes")
+        age_row = sb.tile([P, T], F32, name="age_row")
+        placed = sb.tile([P, T], F32, name="placed")
+        nc.vector.memset(key_bytes[:].bitcast(I32), 0)
+        nc.vector.memset(age_row[:], 0.0)
+        nc.vector.memset(val_bytes[:].bitcast(I32), 0)
+        nc.vector.memset(placed[:], 0.0)
+
+        def load_scale_rows(queue, plane, rows):
+            for quad in range(4):
+                queue.dma_start(
+                    plane[32 * quad : 32 * quad + 4, :].bitcast(I32), rows[0, 4 * quad : 4 * quad + 4, :].bitcast(I32)
+                )
+
+        def load_rows(name, rows):
+            raw = sb.tile([P, PACK, Q], F32, name=name + "_raw")
+            nc.sync.dma_start(raw[:], rows.rearrange("(p j) w -> p j w", j=PACK))
+            return raw
+
+        def load_words(name, words):
+            pool_words = sb.tile([P, T], U16, name=name)
+            nc.sync.dma_start(pool_words[:].bitcast(I32), words[0].bitcast(I32))
+            return pool_words
+
+        identity = sb.tile([P, P], F32, name="identity")
+        make_identity(nc, identity[:])
+        size_cols = sb.tile([P, PACK], F32, name="size_cols")
+        nc.gpsimd.dma_start(size_cols[:], size.rearrange("o (p j) -> (o p) j", j=PACK))
+        grace_col = column("grace_col")
+        nc.gpsimd.dma_start(grace_col[:], grace)
+
+        query_raw = load_rows("query", query)
+        key_words = load_words("key_words", keys_words)
+        load_scale_rows(nc.scalar, key_bytes, keys_scales)
+        query2_raw = load_rows("query2", query2)
+        nc.sync.dma_start(age_row[0:1, :], age[0:1, :])
+        gout_raw = load_rows("gout", gout)
+        dquery2_raw = load_rows("dquery2", dquery2)
+        val_words = load_words("val_words", vals_words)
+        load_scale_rows(nc.sync, val_bytes, vals_scales)
+        base_sb = sb.tile([P, T], F32, name="base_sb")
+        nc.sync.dma_start(base_sb[:], base)
+
+        def interleave(name, raw):
+            grouped = sb.tile([P, Q, PACK], BF16, name=name + "_bf16", align_bytes=64)
+            nc.scalar.activation(
+                grouped[:].rearrange("p (c i) j -> p c j i", i=4), raw[:].rearrange("p j (c i) -> p c j i", i=4), ACT.Copy
+            )
+            return grouped
+
+        def quantise(name, grouped):
+            codes = sb.tile([P, Q], U32, name=name + "_codes", align_bytes=64)
+            scales = sb.tile([P, Q], U8, name=name + "_scales", align_bytes=64)
+            nc.vector.quantize_mx(codes[:].bitcast(FP8X4), scales[:], grouped[:].rearrange("p w j -> p (w j)"))
+            return codes, scales
+
+        def gather(name, window, dtype):
+            picked = sb.tile([P, I], dtype, name=name, align_bytes=64)
+            nc.vector.tensor_copy(picked[:], window[:].indirect(offsets[:]))
+            return picked
+
+        def scores(name, rows, words, scales):
+            acc = ps.tile([Q, I], F32, name=name)
+            nc.tensor.matmul_mx(
+                acc[:], lhsT=rows[0][:].bitcast(FP8X4), lhsT_scale=rows[1][:],
+                rhs=words[:].bitcast(FP4X4), rhs_scale=scales[:], start=True, stop=True,
+            )
+            return acc
+
+        query_bf = interleave("query", query_raw)
+        size_bank = ps.tile([P, PACK, P], F32, name="size_bank")
+        for j in range(PACK):
+            nc.tensor.transpose(size_bank[:, j, :], size_cols[:, j : j + 1].to_broadcast([P, P]), identity[:])
+        query2_bf = interleave("query2", query2_raw)
+        size_wide = wide("size_wide")
+        nc.scalar.activation(
+            size_wide[:].rearrange("q (p j) -> q p j", j=PACK), size_bank[:].rearrange("q j p -> q p j"),
+            ACT.Copy, scale=1536.0,
+        )
+        gout_bf = interleave("gout", gout_raw)
+        dquery2_bf = interleave("dquery2", dquery2_raw)
+
+        key_scales = gather("key_scales", key_bytes, U8)
+        query_mx = quantise("query", query_bf)
+        keys = gather("keys", key_words, U16)
+        query2_mx = quantise("query2", query2_bf)
+        a = scores("a", query_mx, keys, key_scales)
+        b = scores("b", query2_mx, keys, key_scales)
+        ages = gather("ages", age_row, F32)
+        neg_max = column("neg_max")
+        nc.vector.tensor_reduce(neg_max[:], a[:], mybir.AxisListType.X, ALU.max, negate=True)
+
+        graced = wide("graced")
+        nc.scalar.activation(graced[:], b[:], ACT.Identity, bias=grace_col[:])
+        r = wide("r")
+        nc.scalar.activation(r[:], a[:], ACT.Exp, bias=neg_max[:])
+
+        age_turned = ps.tile([P, PACK, P], F32, name="age_turned")
+        for j in range(PACK):
+            nc.tensor.transpose(age_turned[:, j, :], ages[:, j * P : (j + 1) * P], identity[:])
+        age_cols = sb.tile([P, PACK], F32, name="age_cols")
+        nc.vector.tensor_copy(age_cols[:], age_turned[:, :, 0])
+        age_bank = ps.tile([P, PACK, P], F32, name="age_bank")
+        for j in range(PACK):
+            nc.tensor.transpose(age_bank[:, j, :], age_cols[:, j : j + 1].to_broadcast([P, P]), identity[:])
+
+        val_scales = gather("val_scales", val_bytes, U8)
+        logit = wide("logit")
+        nc.vector.tensor_tensor(logit[:], graced[:], age_bank[:].rearrange("q j p -> q (j p)"), ALU.subtract)
+        gout_mx = quantise("gout", gout_bf)
+        dquery2_mx = quantise("dquery2", dquery2_bf)
+        tb = scores("tb", dquery2_mx, keys, key_scales)
+        vals = gather("vals", val_words, U16)
+        c0 = scores("c0", gout_mx, vals, val_scales)
+
+        life = wide("life")
+        nc.scalar.activation(life[:], logit[:], ACT.Sigmoid, scale=3.0)
+        death = wide("death")
+        nc.scalar.activation(death[:], logit[:], ACT.Sigmoid, scale=-3.0)
+        bend = wide("bend")
+        nc.scalar.activation(bend[:], life[:], ACT.Copy, scale=-2.0, bias=1.0)
+
+        p = wide("p")
+        z = column("z")
+        nc.vector.scalar_tensor_tensor(p[:], r[:], 1.0, life[:], ALU.mult, ALU.mult, accum_out=z[:])
+        cs = wide("cs")
+        nc.vector.tensor_tensor(cs[:], c0[:], size_wide[:], ALU.mult)
+        inv_z = column("inv_z")
+        nc.vector.reciprocal(inv_z[:], z[:])
+        h = wide("h")
+        nc.vector.scalar_tensor_tensor(h[:], p[:], inv_z[:], death[:], ALU.mult, ALU.mult)
+        pcs = wide("pcs")
+        mean = column("mean")
+        nc.vector.scalar_tensor_tensor(pcs[:], p[:], inv_z[:], cs[:], ALU.mult, ALU.mult, accum_out=mean[:])
+        tp = wide("tp")
+        tau = column("tau")
+        nc.vector.scalar_tensor_tensor(tp[:], tb[:], 3.0, h[:], ALU.mult, ALU.mult, accum_out=tau[:])
+        centred = wide("centred")
+        nc.scalar.activation(centred[:], cs[:], ACT.Identity, scale=-1.0, bias=mean[:])
+        moved = wide("moved")
+        beta = column("beta")
+        nc.vector.scalar_tensor_tensor(moved[:], cs[:], mean[:], tp[:], ALU.subtract, ALU.mult, accum_out=beta[:])
+        shift = wide("shift")
+        nc.scalar.activation(shift[:], centred[:], ACT.Copy, scale=tau[:])
+        first = wide("first")
+        nc.vector.tensor_tensor(first[:], moved[:], bend[:], ALU.mult)
+        second = wide("second")
+        nc.vector.scalar_tensor_tensor(second[:], shift[:], beta[:], h[:], ALU.subtract, ALU.mult)
+        nc.vector.tensor_tensor(placed[:].indirect(offsets[:]), first[:], second[:], ALU.add)
+
+        for lo, hi in zip(STORE_EDGES[:-1], STORE_EDGES[1:]):
+            result = sb.tile([P, hi - lo], F32, name="result%d" % lo)
+            nc.vector.tensor_tensor(result[:], base_sb[:, lo:hi], placed[:, lo:hi], ALU.add)
+            nc.sync.dma_start(out[:, lo:hi], result[:])

@@ -6,7 +6,7 @@ from concourse.masks import make_identity
 D, T, I, Q = 512, 2048, 512, 128
 P = 128
 PACK = 4
-STORE_EDGES = (0, 256, 768, 1280, 1792, 2048)
+STORE_EDGES = (0, 320, 832, 1344, 1920, 2048)
 
 FLOPS = 4 * 2 * D * Q * I
 
@@ -43,10 +43,9 @@ def tile_attend_hvsoftlives_b_s_kernel(
         val_bytes = sb.tile([P, T], U8, name="val_bytes")
         age_row = sb.tile([P, T], F32, name="age_row")
         placed = sb.tile([P, T], F32, name="placed")
-        nc.vector.memset(key_bytes[:].bitcast(I32), 0)
-        nc.vector.memset(age_row[:], 0.0)
+        nc.gpsimd.memset(key_bytes[:].bitcast(I32), 0)
         nc.vector.memset(val_bytes[:].bitcast(I32), 0)
-        nc.vector.memset(placed[:], 0.0)
+        nc.vector.memset(placed[:].bitcast(I32), 0)
 
         def load_scale_rows(queue, plane, rows):
             for quad in range(4):
@@ -64,27 +63,27 @@ def tile_attend_hvsoftlives_b_s_kernel(
             nc.sync.dma_start(pool_words[:].bitcast(I32), words[0].bitcast(I32))
             return pool_words
 
-        identity = sb.tile([P, P], F32, name="identity")
-        make_identity(nc, identity[:])
         size_cols = sb.tile([P, PACK], F32, name="size_cols")
         nc.gpsimd.dma_start(size_cols[:], size.rearrange("o (p j) -> (o p) j", j=PACK))
+        identity = sb.tile([P, P], F32, name="identity")
+        make_identity(nc, identity[:])
         grace_col = column("grace_col")
         nc.gpsimd.dma_start(grace_col[:], grace)
 
-        query_raw = load_rows("query", query)
+        load_scale_rows(nc.sync, key_bytes, keys_scales)
         key_words = load_words("key_words", keys_words)
-        load_scale_rows(nc.scalar, key_bytes, keys_scales)
+        query_raw = load_rows("query", query)
         query2_raw = load_rows("query2", query2)
-        nc.sync.dma_start(age_row[0:1, :], age[0:1, :])
         gout_raw = load_rows("gout", gout)
         dquery2_raw = load_rows("dquery2", dquery2)
-        val_words = load_words("val_words", vals_words)
         load_scale_rows(nc.sync, val_bytes, vals_scales)
+        nc.sync.dma_start(age_row[:], age)
+        val_words = load_words("val_words", vals_words)
         base_sb = sb.tile([P, T], F32, name="base_sb")
         nc.sync.dma_start(base_sb[:], base)
 
-        def interleave(name, raw):
-            grouped = sb.tile([P, Q, PACK], BF16, name=name + "_bf16", align_bytes=64)
+        def interleave(name, raw, tag=""):
+            grouped = sb.tile([P, Q, PACK], BF16, name=name + "_bf16", align_bytes=64, tag=tag)
             nc.scalar.activation(
                 grouped[:].rearrange("p (c i) j -> p c j i", i=4), raw[:].rearrange("p j (c i) -> p c j i", i=4), ACT.Copy
             )
@@ -96,8 +95,8 @@ def tile_attend_hvsoftlives_b_s_kernel(
             nc.vector.quantize_mx(codes[:].bitcast(FP8X4), scales[:], grouped[:].rearrange("p w j -> p (w j)"))
             return codes, scales
 
-        def gather(name, window, dtype):
-            picked = sb.tile([P, I], dtype, name=name, align_bytes=64)
+        def gather(name, window, dtype, tag=""):
+            picked = sb.tile([P, I], dtype, name=name, align_bytes=64, tag=tag)
             nc.vector.tensor_copy(picked[:], window[:].indirect(offsets[:]))
             return picked
 
@@ -113,67 +112,58 @@ def tile_attend_hvsoftlives_b_s_kernel(
         size_bank = ps.tile([P, PACK, P], F32, name="size_bank")
         for j in range(PACK):
             nc.tensor.transpose(size_bank[:, j, :], size_cols[:, j : j + 1].to_broadcast([P, P]), identity[:])
-        query2_bf = interleave("query2", query2_raw)
         size_wide = wide("size_wide")
         nc.scalar.activation(
             size_wide[:].rearrange("q (p j) -> q p j", j=PACK), size_bank[:].rearrange("q j p -> q p j"),
             ACT.Copy, scale=1536.0,
         )
+        query2_bf = interleave("query2", query2_raw)
         gout_bf = interleave("gout", gout_raw)
         dquery2_bf = interleave("dquery2", dquery2_raw)
 
-        key_scales = gather("key_scales", key_bytes, U8)
-        query_mx = quantise("query", query_bf)
         keys = gather("keys", key_words, U16)
+        query_mx = quantise("query", query_bf)
+        key_scales = gather("key_scales", key_bytes, U8)
         query2_mx = quantise("query2", query2_bf)
         a = scores("a", query_mx, keys, key_scales)
         b = scores("b", query2_mx, keys, key_scales)
-        ages = gather("ages", age_row, F32)
+        gout_mx = quantise("gout", gout_bf)
         neg_max = column("neg_max")
         nc.vector.tensor_reduce(neg_max[:], a[:], mybir.AxisListType.X, ALU.max, negate=True)
-
         graced = wide("graced")
         nc.scalar.activation(graced[:], b[:], ACT.Identity, bias=grace_col[:])
         r = wide("r")
         nc.scalar.activation(r[:], a[:], ACT.Exp, bias=neg_max[:])
 
-        age_turned = ps.tile([P, PACK, P], F32, name="age_turned")
-        for j in range(PACK):
-            nc.tensor.transpose(age_turned[:, j, :], ages[:, j * P : (j + 1) * P], identity[:])
-        age_cols = sb.tile([P, PACK], F32, name="age_cols")
-        nc.vector.tensor_copy(age_cols[:], age_turned[:, :, 0])
-        age_bank = ps.tile([P, PACK, P], F32, name="age_bank")
-        for j in range(PACK):
-            nc.tensor.transpose(age_bank[:, j, :], age_cols[:, j : j + 1].to_broadcast([P, P]), identity[:])
-
-        val_scales = gather("val_scales", val_bytes, U8)
-        logit = wide("logit")
-        nc.vector.tensor_tensor(logit[:], graced[:], age_bank[:].rearrange("q j p -> q (j p)"), ALU.subtract)
-        gout_mx = quantise("gout", gout_bf)
         dquery2_mx = quantise("dquery2", dquery2_bf)
         tb = scores("tb", dquery2_mx, keys, key_scales)
+        val_scales = gather("val_scales", val_bytes, U8)
+        overdue = wide("overdue")
+        nc.vector.tensor_tensor(overdue[:], age_row[:].indirect(offsets[:]), graced[:], ALU.subtract)
         vals = gather("vals", val_words, U16)
         c0 = scores("c0", gout_mx, vals, val_scales)
 
         life = wide("life")
-        nc.scalar.activation(life[:], logit[:], ACT.Sigmoid, scale=3.0)
+        nc.scalar.activation(life[:], overdue[:], ACT.Sigmoid, scale=-3.0)
         death = wide("death")
-        nc.scalar.activation(death[:], logit[:], ACT.Sigmoid, scale=-3.0)
+        nc.scalar.activation(death[:], overdue[:], ACT.Sigmoid, scale=3.0)
         bend = wide("bend")
         nc.scalar.activation(bend[:], life[:], ACT.Copy, scale=-2.0, bias=1.0)
 
         p = wide("p")
         z = column("z")
         nc.vector.scalar_tensor_tensor(p[:], r[:], 1.0, life[:], ALU.mult, ALU.mult, accum_out=z[:])
-        cs = wide("cs")
+        cs = r
         nc.vector.tensor_tensor(cs[:], c0[:], size_wide[:], ALU.mult)
         inv_z = column("inv_z")
         nc.vector.reciprocal(inv_z[:], z[:])
+        pcs = wide("pcs")
+        weighted = column("weighted")
+        nc.vector.scalar_tensor_tensor(pcs[:], p[:], 1.0, cs[:], ALU.mult, ALU.mult, accum_out=weighted[:])
         h = wide("h")
         nc.vector.scalar_tensor_tensor(h[:], p[:], inv_z[:], death[:], ALU.mult, ALU.mult)
-        pcs = wide("pcs")
         mean = column("mean")
-        nc.vector.scalar_tensor_tensor(pcs[:], p[:], inv_z[:], cs[:], ALU.mult, ALU.mult, accum_out=mean[:])
+        nc.vector.tensor_tensor(mean[:], weighted[:], inv_z[:], ALU.mult)
         tp = wide("tp")
         tau = column("tau")
         nc.vector.scalar_tensor_tensor(tp[:], tb[:], 3.0, h[:], ALU.mult, ALU.mult, accum_out=tau[:])

from contextlib import ExitStack

import concourse.mybir as mybir
from concourse.masks import make_identity

D, T, I, Q = 512, 2048, 512, 128
P = 128
PACK = 4
STORE_EDGES = (0, 320, 832, 1344, 1920, 2048)

FLOPS = 4 * 2 * D * Q * I

F32 = mybir.dt.float32
BF16 = mybir.dt.bfloat16
I32 = mybir.dt.int32
U32 = mybir.dt.uint32
U16 = mybir.dt.uint16
U8 = mybir.dt.uint8
FP8X4 = mybir.dt.float8_e4m3fn_x4
FP4X4 = mybir.dt.float4_e2m1fn_x4
ALU = mybir.AluOpType
ACT = mybir.ActivationFunctionType


def tile_attend_hvsoftlives_b_s_kernel(
    tc, query, query2, keys_words, keys_scales, age, grace, gout, vals_words, vals_scales, size, dquery2, base, offs, out
):
    nc = tc.nc
    with ExitStack() as ctx:
        sb = ctx.enter_context(tc.tile_pool(name="sb", bufs=1))
        ps = ctx.enter_context(tc.psum_pool(name="ps", bufs=1))

        def wide(name):
            return sb.tile([P, I], F32, name=name)

        def column(name):
            return sb.tile([P, 1], F32, name=name)

        offsets = sb.tile([P, I // 16], U16, name="offsets")
        nc.sync.dma_start(offsets[:], offs)

        key_bytes = sb.tile([P, T], U8, name="key_bytes")
        val_bytes = sb.tile([P, T], U8, name="val_bytes")
        age_row = sb.tile([P, T], F32, name="age_row")
        placed = sb.tile([P, T], F32, name="placed")
        nc.gpsimd.memset(key_bytes[:].bitcast(I32), 0)
        nc.vector.memset(val_bytes[:].bitcast(I32), 0)
        nc.vector.memset(placed[:].bitcast(I32), 0)

        def load_scale_rows(queue, plane, rows):
            for quad in range(4):
                queue.dma_start(
                    plane[32 * quad : 32 * quad + 4, :].bitcast(I32), rows[0, 4 * quad : 4 * quad + 4, :].bitcast(I32)
                )

        def load_rows(name, rows):
            raw = sb.tile([P, PACK, Q], F32, name=name + "_raw")
            nc.sync.dma_start(raw[:], rows.rearrange("(p j) w -> p j w", j=PACK))
            return raw

        def load_words(name, words):
            pool_words = sb.tile([P, T], U16, name=name)
            nc.sync.dma_start(pool_words[:].bitcast(I32), words[0].bitcast(I32))
            return pool_words

        size_cols = sb.tile([P, PACK], F32, name="size_cols")
        nc.gpsimd.dma_start(size_cols[:], size.rearrange("o (p j) -> (o p) j", j=PACK))
        identity = sb.tile([P, P], F32, name="identity")
        make_identity(nc, identity[:])
        grace_col = column("grace_col")
        nc.gpsimd.dma_start(grace_col[:], grace)

        load_scale_rows(nc.sync, key_bytes, keys_scales)
        key_words = load_words("key_words", keys_words)
        query_raw = load_rows("query", query)
        query2_raw = load_rows("query2", query2)
        gout_raw = load_rows("gout", gout)
        dquery2_raw = load_rows("dquery2", dquery2)
        load_scale_rows(nc.sync, val_bytes, vals_scales)
        nc.sync.dma_start(age_row[:], age)
        val_words = load_words("val_words", vals_words)
        base_sb = sb.tile([P, T], F32, name="base_sb")
        nc.sync.dma_start(base_sb[:], base)

        def interleave(name, raw, tag=""):
            grouped = sb.tile([P, Q, PACK], BF16, name=name + "_bf16", align_bytes=64, tag=tag)
            nc.scalar.activation(
                grouped[:].rearrange("p (c i) j -> p c j i", i=4), raw[:].rearrange("p j (c i) -> p c j i", i=4), ACT.Copy
            )
            return grouped

        def quantise(name, grouped):
            codes = sb.tile([P, Q], U32, name=name + "_codes", align_bytes=64)
            scales = sb.tile([P, Q], U8, name=name + "_scales", align_bytes=64)
            nc.vector.quantize_mx(codes[:].bitcast(FP8X4), scales[:], grouped[:].rearrange("p w j -> p (w j)"))
            return codes, scales

        def gather(name, window, dtype, tag=""):
            picked = sb.tile([P, I], dtype, name=name, align_bytes=64, tag=tag)
            nc.vector.tensor_copy(picked[:], window[:].indirect(offsets[:]))
            return picked

        def scores(name, rows, words, scales):
            acc = ps.tile([Q, I], F32, name=name)
            nc.tensor.matmul_mx(
                acc[:], lhsT=rows[0][:].bitcast(FP8X4), lhsT_scale=rows[1][:],
                rhs=words[:].bitcast(FP4X4), rhs_scale=scales[:], start=True, stop=True,
            )
            return acc

        query_bf = interleave("query", query_raw)
        size_bank = ps.tile([P, PACK, P], F32, name="size_bank")
        for j in range(PACK):
            nc.tensor.transpose(size_bank[:, j, :], size_cols[:, j : j + 1].to_broadcast([P, P]), identity[:])
        size_wide = wide("size_wide")
        nc.scalar.activation(
            size_wide[:].rearrange("q (p j) -> q p j", j=PACK), size_bank[:].rearrange("q j p -> q p j"),
            ACT.Copy, scale=1536.0,
        )
        query2_bf = interleave("query2", query2_raw)
        gout_bf = interleave("gout", gout_raw)
        dquery2_bf = interleave("dquery2", dquery2_raw)

        keys = gather("keys", key_words, U16)
        query_mx = quantise("query", query_bf)
        key_scales = gather("key_scales", key_bytes, U8)
        query2_mx = quantise("query2", query2_bf)
        a = scores("a", query_mx, keys, key_scales)
        b = scores("b", query2_mx, keys, key_scales)
        gout_mx = quantise("gout", gout_bf)
        neg_max = column("neg_max")
        nc.vector.tensor_reduce(neg_max[:], a[:], mybir.AxisListType.X, ALU.max, negate=True)
        graced = wide("graced")
        nc.scalar.activation(graced[:], b[:], ACT.Identity, bias=grace_col[:])
        r = wide("r")
        nc.scalar.activation(r[:], a[:], ACT.Exp, bias=neg_max[:])

        dquery2_mx = quantise("dquery2", dquery2_bf)
        tb = scores("tb", dquery2_mx, keys, key_scales)
        val_scales = gather("val_scales", val_bytes, U8)
        overdue = wide("overdue")
        nc.vector.tensor_tensor(overdue[:], age_row[:].indirect(offsets[:]), graced[:], ALU.subtract)
        vals = gather("vals", val_words, U16)
        c0 = scores("c0", gout_mx, vals, val_scales)

        life = wide("life")
        nc.scalar.activation(life[:], overdue[:], ACT.Sigmoid, scale=-3.0)
        death = wide("death")
        nc.scalar.activation(death[:], overdue[:], ACT.Sigmoid, scale=3.0)
        bend = wide("bend")
        nc.scalar.activation(bend[:], life[:], ACT.Copy, scale=-2.0, bias=1.0)

        p = wide("p")
        z = column("z")
        nc.vector.scalar_tensor_tensor(p[:], r[:], 1.0, life[:], ALU.mult, ALU.mult, accum_out=z[:])
        cs = r
        nc.vector.tensor_tensor(cs[:], c0[:], size_wide[:], ALU.mult)
        inv_z = column("inv_z")
        nc.vector.reciprocal(inv_z[:], z[:])
        pcs = wide("pcs")
        weighted = column("weighted")
        nc.vector.scalar_tensor_tensor(pcs[:], p[:], 1.0, cs[:], ALU.mult, ALU.mult, accum_out=weighted[:])
        h = wide("h")
        nc.vector.scalar_tensor_tensor(h[:], p[:], inv_z[:], death[:], ALU.mult, ALU.mult)
        mean = column("mean")
        nc.vector.tensor_tensor(mean[:], weighted[:], inv_z[:], ALU.mult)
        tp = wide("tp")
        tau = column("tau")
        nc.vector.scalar_tensor_tensor(tp[:], tb[:], 3.0, h[:], ALU.mult, ALU.mult, accum_out=tau[:])
        centred = wide("centred")
        nc.scalar.activation(centred[:], cs[:], ACT.Identity, scale=-1.0, bias=mean[:])
        moved = wide("moved")
        beta = column("beta")
        nc.vector.scalar_tensor_tensor(moved[:], cs[:], mean[:], tp[:], ALU.subtract, ALU.mult, accum_out=beta[:])
        shift = wide("shift")
        nc.scalar.activation(shift[:], centred[:], ACT.Copy, scale=tau[:])
        first = wide("first")
        nc.vector.tensor_tensor(first[:], moved[:], bend[:], ALU.mult)
        second = wide("second")
        nc.vector.scalar_tensor_tensor(second[:], shift[:], beta[:], h[:], ALU.subtract, ALU.mult)
        nc.vector.tensor_tensor(placed[:].indirect(offsets[:]), first[:], second[:], ALU.add)

        for lo, hi in zip(STORE_EDGES[:-1], STORE_EDGES[1:]):
            result = sb.tile([P, hi - lo], F32, name="result%d" % lo)
            nc.vector.tensor_tensor(result[:], base_sb[:, lo:hi], placed[:, lo:hi], ALU.add)
            nc.sync.dma_start(out[:, lo:hi], result[:])
